import numpy as np
import ml_dtypes


def mxq(x, axis, fmt="e4m3"):
    dtype, down = {"e4m3": (ml_dtypes.float8_e4m3fn, 7), "e5m2": (ml_dtypes.float8_e5m2, 14)}[fmt]
    v = np.moveaxis(np.asarray(x, np.float32).astype(ml_dtypes.bfloat16).astype(np.float64), axis, -1)
    blocks = v.reshape(v.shape[:-1] + (-1, 32))
    amax = np.abs(blocks).max(-1, keepdims=True)
    byte = np.maximum(np.where(amax > 0, np.frexp(amax)[1] - 1 + 127, 0) - down, 1)
    scale = np.exp2(byte - 127.0)
    codes = (blocks / scale).astype(np.float32).astype(dtype).astype(np.float64)
    return np.moveaxis((codes * scale).reshape(v.shape), -1, axis)


WIDE = False


def mx_kscale(k):
    if not WIDE:
        return np.ones(k)
    levels = np.array([10, -10, 5, -5, 0])
    if k % 512:
        return np.exp2(np.random.permutation(np.resize(levels, k // 32))).repeat(32)
    a = np.empty((k // 512, 16))
    for p in range(k // 512):
        a[p, :8] = np.random.permutation(np.resize(levels, 8))
        for g in range(8):
            far = levels[np.abs(levels - a[p, g]) >= 10]
            a[p, g + 8] = far[np.random.randint(len(far))]
    return np.exp2(a.ravel()).repeat(32)


def f64(x):
    return np.asarray(x).astype(np.float64)


def striped8(idx):
    return np.asarray(idx).reshape(8, -1, 16).transpose(0, 2, 1).reshape(128, -1).astype(np.uint16)


def unstriped8(offs):
    return offs.reshape(8, 16, -1).transpose(0, 2, 1).reshape(8, -1).astype(np.int64)


def pick8(x, idx, run):
    r = np.arange(len(x))
    return x[r[:, None], idx[r % (8 * run) // run]]


E2M1 = np.array([0.0, 0.5, 1.0, 1.5, 2.0, 3.0, 4.0, 6.0, -0.0, -0.5, -1.0, -1.5, -2.0, -3.0, -4.0, -6.0])


def pack_weight(w, fmt):
    k, n = w.shape
    w = f64(np.asarray(w, np.float32).astype(ml_dtypes.bfloat16)).reshape(k // 32, 32, n)
    amax = np.abs(w).max(1)
    if fmt == "e4m3":
        byte = np.frexp(amax)[1] - 1 + 127 - 7
    else:
        mant, ex = np.frexp(amax / 6.0)
        byte = np.where(mant > 0.5, ex, ex - 1) + 127
    byte = np.clip(np.where(amax > 0, byte, 1), 1, 254)
    scaled = (w * np.exp2(127.0 - byte)[:, None, :]).reshape(k, n).astype(np.float32)
    by_word = np.ascontiguousarray(scaled.reshape(k // 512, 128, 4, n).transpose(0, 1, 3, 2))
    if fmt == "e4m3":
        words = by_word.astype(ml_dtypes.float8_e4m3fn).view(np.uint8)
    else:
        c = by_word.astype(ml_dtypes.float4_e2m1fn).view(np.uint8) & 0xF
        words = (c[..., 0::2] | (c[..., 1::2] << 4)).reshape(k // 512, 128, 2 * n)
    return np.ascontiguousarray(words), np.ascontiguousarray(byte.astype(np.uint8).reshape(k // 512, 16, n))


def unpack_weight(words, scales, fmt):
    g, _, n = scales.shape
    words = np.ascontiguousarray(words).reshape(g, 128, n, -1)
    if fmt == "e4m3":
        vals = words.view(ml_dtypes.float8_e4m3fn).astype(np.float64)
    else:
        nib = np.empty((g, 128, n, 4), np.uint8)
        nib[..., 0::2] = words & 0xF
        nib[..., 1::2] = words >> 4
        vals = E2M1[nib]
    vals = vals * np.repeat(np.exp2(scales.astype(np.float64) - 127.0), 8, axis=1)[..., None]
    return vals.transpose(0, 1, 3, 2).reshape(g * 512, n)


D, T, I, Q = 512, 1024, 512, 128


def setup_inputs():
    n = np.random.standard_normal
    idx = np.stack([np.random.permutation(T)[:I] for _ in range(8)])
    idx2 = np.stack([np.random.permutation(T)[:I] for _ in range(8)])
    idx3 = np.stack([np.random.permutation(T)[:I] for _ in range(8)])
    fd = mx_kscale(D)
    keysp = pack_weight(n((D, T)) / fd[:, None], "e4m3")
    return {
        "query": (n((D, Q)) * 0.9 / np.sqrt(D) * fd[:, None]).astype(np.float32),
        "query2": (n((D, Q)) * 0.9 / np.sqrt(D) * fd[:, None]).astype(np.float32),
        "keys_words": keysp[0],
        "keys_scales": keysp[1],
        "lam": (np.random.uniform(1.0, 2.5, (Q, 1))).astype(np.float32),
        "pull": (np.random.uniform(0.3, 0.9, (Q, 1))).astype(np.float32),
        "old": (np.random.uniform(0.0, 2.0, (Q, T))).astype(np.float32),
        "fade": (np.random.uniform(0.3, 0.9, (Q, 1))).astype(np.float32),
        "offs": striped8(idx),
        "offs2": striped8(idx2),
        "offs3": striped8(idx3),
    }


def reference(query, query2, keys_words, keys_scales, lam, pull, old, fade, offs, offs2, offs3):
    idx = unstriped8(offs)
    idx2 = unstriped8(offs2)
    idx3 = unstriped8(offs3)
    keysu = unpack_weight(keys_words, keys_scales, "e4m3")
    queryq = mxq(f64(query), 0, "e4m3")
    a = queryq.T @ keysu
    query2q = mxq(f64(query2), 0, "e4m3")
    b = query2q.T @ keysu
    e1s = np.exp(pick8(a, idx, 16))
    s = e1s / (e1s + np.exp(pick8(a, idx2, 16)) + np.exp(pick8(b, idx3, 16))) * f64(lam)
    p = np.exp(s - np.max(s, axis=1, keepdims=True))
    r = p / np.sum(p, axis=1, keepdims=True)
    r1 = np.pad(r, ((0, 0), (1, 0)))[:, :I]
    w = r - r1 * f64(pull)
    ws = w * 256.0
    wf = np.zeros((Q, T))
    wf[np.arange(Q)[:, None], idx[np.arange(Q) % 128 // 16]] = ws
    y = f64(old) * f64(fade) + wf
    return y

@@ -1,0 +1,211 @@
+from contextlib import ExitStack
+
+import concourse.mybir as mybir
+
+D, T, I, Q = 512, 1024, 512, 128
+FLOPS = 2 * 2 * D * T * Q
+
+F32 = mybir.dt.float32
+BF16 = mybir.dt.bfloat16
+I32 = mybir.dt.int32
+U32 = mybir.dt.uint32
+U16 = mybir.dt.uint16
+U8 = mybir.dt.uint8
+FP8X4 = mybir.dt.float8_e4m3fn_x4
+ALU = mybir.AluOpType
+ACT = mybir.ActivationFunctionType
+AX = mybir.AxisListType
+
+P = 128
+PACK = 4
+NB = 256
+HALF = I // 2
+QUART = HALF // 4
+CAP = 2.0 ** 30
+OUTC = 256
+
+
+def tile_attend_quotaratio_stepwise_counts_heads_kernel(
+    tc, query, query2, keys_words, keys_scales, lam, pull, old, fade, offs, offs2, offs3, out
+):
+    nc = tc.nc
+    with ExitStack() as ctx:
+        sb = ctx.enter_context(tc.tile_pool(name="sb", bufs=1))
+        ps = ctx.enter_context(tc.psum_pool(name="ps", bufs=1))
+
+        list1 = sb.tile([P, I // 16], U16, name="list1")
+        list2 = sb.tile([P, I // 16], U16, name="list2")
+        list3 = sb.tile([P, I // 16], U16, name="list3")
+        key_words = [sb.tile([P, T // 2], U32, name="key_words%d" % j, align_bytes=64) for j in range(2)]
+        key_scales = sb.tile([P, T], U8, name="key_scales", align_bytes=64)
+        raw = [sb.tile([P, PACK, Q], F32, name="raw%d" % j) for j in range(2)]
+        lam_t = sb.tile([P, 1], F32, name="lam_t")
+        pull_t = sb.tile([P, 1], F32, name="pull_t")
+        fade_t = sb.tile([P, 1], F32, name="fade_t")
+        old_t = sb.tile([P, T], F32, name="old_t")
+        placed = sb.tile([P, T], F32, name="placed")
+        p_pad = sb.tile([P, I + 1], F32, name="p_pad")
+
+        nc.vector.memset(key_scales[:].bitcast(I32), 0)
+        nc.sync.dma_start(out=raw[0][:], in_=query.rearrange("(p j) w -> p j w", j=PACK))
+        for g in range(4):
+            nc.scalar.dma_start(
+                out=key_scales[32 * g : 32 * g + 4, :].bitcast(I32),
+                in_=keys_scales[0, 4 * g : 4 * g + 4, :].bitcast(I32),
+            )
+        words_hbm = keys_words[0].rearrange("p n t -> p (n t)").bitcast(I32)
+        nc.sync.dma_start(out=key_words[0][:].bitcast(I32), in_=words_hbm[:, 0 : T // 2])
+        nc.sync.dma_start(out=raw[1][:], in_=query2.rearrange("(p j) w -> p j w", j=PACK))
+        nc.sync.dma_start(out=key_words[1][:].bitcast(I32), in_=words_hbm[:, T // 2 : T])
+        nc.sync.dma_start(list1[:], offs)
+        nc.sync.dma_start(list2[:], offs2)
+        nc.sync.dma_start(list3[:], offs3)
+        nc.gpsimd.dma_start(out=pull_t[:], in_=pull)
+        nc.gpsimd.dma_start(out=lam_t[:], in_=lam)
+        nc.gpsimd.dma_start(out=fade_t[:], in_=fade)
+        nc.sync.dma_start(out=old_t[:], in_=old)
+        nc.vector.memset(placed[:], 0.0)
+        nc.vector.memset(p_pad[:, 0:1], 0.0)
+
+        neg_pull = sb.tile([P, 1], F32, name="neg_pull")
+        nc.scalar.activation(neg_pull[:], pull_t[:], ACT.Copy, scale=-1.0)
+        half_sign = sb.tile([P, 1], F32, name="half_sign")
+        nc.gpsimd.tensor_scalar(half_sign[:], lam_t[:], 0.0, -0.5, ALU.is_ge, ALU.add)
+        gain = sb.tile([P, 1], F32, name="gain")
+        nc.gpsimd.tensor_tensor(gain[:], lam_t[:], half_sign[:], ALU.mult)
+        neg_gain = sb.tile([P, 1], F32, name="neg_gain")
+        nc.gpsimd.tensor_scalar(neg_gain[:], gain[:], -1.0, 0.0, ALU.mult, ALU.add)
+
+        scores = []
+        for j in range(2):
+            grouped = sb.tile([P, Q, PACK], BF16, name="grouped%d" % j, align_bytes=64)
+            nc.vector.tensor_copy(
+                out=grouped[:].rearrange("p (c i) t -> p c t i", i=4),
+                in_=raw[j][:].rearrange("p t (c i) -> p c t i", i=4),
+            )
+            codes = sb.tile([P, Q], U32, name="codes%d" % j, align_bytes=64)
+            qscales = sb.tile([P, Q], U8, name="qscales%d" % j, align_bytes=64)
+            nc.vector.quantize_mx(
+                out=codes[:].bitcast(FP8X4), scales=qscales[:], in_=grouped[:].rearrange("p w j -> p (w j)")
+            )
+            whole = sb.tile([P, T], F32, name="whole%d" % j)
+            for n in range(T // NB):
+                cols = slice(n * NB, (n + 1) * NB)
+                bank = ps.tile([P, NB], F32, name="bank%d_%d" % (j, n))
+                nc.tensor.matmul_mx(
+                    out=bank[:],
+                    lhsT=codes[:].bitcast(FP8X4),
+                    lhsT_scale=qscales[:],
+                    rhs=key_words[n // 2][:, (n % 2) * NB : (n % 2 + 1) * NB].bitcast(FP8X4),
+                    rhs_scale=key_scales[:, cols],
+                    start=True,
+                    stop=True,
+                )
+                if j == 0 and n % 2 == 1:
+                    nc.vector.tensor_copy(out=whole[:, cols], in_=bank[:])
+                else:
+                    nc.scalar.copy(whole[:, cols], bank[:])
+            scores.append(whole)
+        a, b = scores
+
+        def entries(lst, h):
+            return lst[:, h * (HALF // 16) : (h + 1) * (HALF // 16)]
+
+        own = [sb.tile([P, HALF], F32, name="own%d" % h) for h in range(2)]
+        diff = [sb.tile([P, 2, HALF], F32, name="diff%d" % h) for h in range(2)]
+        ex = [sb.tile([P, 2, HALF], F32, name="ex%d" % h) for h in range(2)]
+        third = sb.tile([P, HALF], F32, name="third")
+
+        nc.vector.tensor_copy(own[0][:], a[:].indirect(entries(list1, 0)))
+        nc.vector.tensor_tensor(diff[0][:, 0, :], a[:].indirect(entries(list2, 0)), own[0][:], ALU.subtract)
+        nc.scalar.activation(own[1][:], a[:].indirect(entries(list1, 1)), ACT.Copy)
+        nc.vector.tensor_tensor(diff[0][:, 1, :], b[:].indirect(entries(list3, 0)), own[0][:], ALU.subtract)
+        nc.scalar.activation(ex[0][:, 0, :], diff[0][:, 0, :], ACT.Exp)
+        nc.scalar.activation(ex[0][:, 1, :], diff[0][:, 1, :], ACT.Exp)
+        nc.vector.tensor_tensor(diff[1][:, 0, :], a[:].indirect(entries(list2, 1)), own[1][:], ALU.subtract)
+        nc.scalar.activation(third[:], b[:].indirect(entries(list3, 1)), ACT.Copy)
+        nc.scalar.activation(ex[1][:, 0, :], diff[1][:, 0, :], ACT.Exp)
+
+        den = sb.tile([P, I], F32, name="den")
+        total = [sb.tile([P, HALF], F32, name="total%d" % h) for h in range(2)]
+        pair = [sb.tile([P, 2, QUART], F32, name="pair%d" % h) for h in range(2)]
+        quad = [sb.tile([P, QUART + h], F32, name="quad%d" % h) for h in range(2)]
+        inv_quad = [sb.tile([P, QUART + h], F32, name="inv_quad%d" % h) for h in range(2)]
+        inv_pair = [sb.tile([P, 2, QUART], F32, name="inv_pair%d" % h) for h in range(2)]
+        inv_den = [sb.tile([P, 2, 2 * QUART], F32, name="inv_den%d" % h) for h in range(2)]
+
+        def den_half(h):
+            return den[:, h * HALF : (h + 1) * HALF].rearrange("p (u n) -> p u n", u=2)
+
+        def make_den(h):
+            nc.vector.scalar_tensor_tensor(total[h][:], ex[h][:, 0, :], 1.0, ex[h][:, 1, :], ALU.add, ALU.add)
+            nc.vector.tensor_scalar(den[:, h * HALF : (h + 1) * HALF], total[h][:], CAP, half_sign[:], ALU.min, ALU.mult)
+
+        def fold(h):
+            dh = den_half(h)
+            nc.vector.tensor_tensor(pair[h][:].rearrange("p v n -> p (v n)"), dh[:, 0, :], dh[:, 1, :], ALU.mult)
+            nc.vector.tensor_tensor(quad[h][:, 0:QUART], pair[h][:, 0, :], pair[h][:, 1, :], ALU.mult)
+
+        def unfold(h):
+            nc.vector.tensor_tensor(
+                inv_pair[h][:],
+                inv_quad[h][:, 0:QUART].unsqueeze(1).to_broadcast([P, 2, QUART]),
+                pair[h][:, ::-1, :],
+                ALU.mult,
+            )
+            nc.vector.tensor_tensor(
+                inv_den[h][:],
+                inv_pair[h][:].rearrange("p v n -> p (v n)").unsqueeze(1).to_broadcast([P, 2, 2 * QUART]),
+                den_half(h)[:, ::-1, :],
+                ALU.mult,
+            )
+
+        make_den(0)
+        nc.vector.tensor_tensor(diff[1][:, 1, :], third[:], own[1][:], ALU.subtract)
+        nc.scalar.activation(ex[1][:, 1, :], diff[1][:, 1, :], ACT.Exp)
+        fold(0)
+        nc.vector.reciprocal(inv_quad[0][:], quad[0][:])
+        make_den(1)
+        fold(1)
+        nc.vector.tensor_reduce(quad[1][:, QUART : QUART + 1], den[:], AX.X, ALU.min)
+        unfold(0)
+        nc.vector.reciprocal(inv_quad[1][:], quad[1][:])
+        neg_max = sb.tile([P, 1], F32, name="neg_max")
+        nc.scalar.activation(neg_max[:], inv_quad[1][:, QUART : QUART + 1], ACT.Copy, scale=neg_gain[:])
+        unfold(1)
+
+        sums = sb.tile([P, 2], F32, name="sums")
+        step = [sb.tile([P, HALF], F32, name="step%d" % h) for h in range(2)]
+        for h in range(2):
+            nc.scalar.activation(
+                p_pad[:, 1 + h * HALF : 1 + (h + 1) * HALF],
+                inv_den[h][:].rearrange("p u n -> p (u n)"),
+                ACT.Exp,
+                bias=neg_max[:],
+                scale=gain[:],
+                accum_out=sums[:, h : h + 1],
+            )
+            nc.vector.scalar_tensor_tensor(
+                step[h][:],
+                p_pad[:, h * HALF : (h + 1) * HALF],
+                neg_pull[:],
+                p_pad[:, 1 + h * HALF : 1 + (h + 1) * HALF],
+                ALU.mult,
+                ALU.add,
+            )
+        row_sum = sb.tile([P, 1], F32, name="row_sum")
+        nc.vector.tensor_scalar(row_sum[:], sums[:, 0:1], sums[:, 1:2], 1.0 / 256.0, ALU.add, ALU.mult)
+        norm = sb.tile([P, 1], F32, name="norm")
+        nc.vector.reciprocal(norm[:], row_sum[:])
+        ws = [sb.tile([P, HALF], F32, name="ws%d" % h) for h in range(2)]
+        nc.vector.tensor_scalar(ws[0][:], step[0][:], norm[:], None, ALU.mult)
+        nc.scalar.activation(ws[1][:], step[1][:], ACT.Copy, scale=norm[:])
+        for h in range(2):
+            nc.vector.tensor_copy(placed[:].indirect(entries(list1, h)), ws[h][:])
+
+        for n in range(T // OUTC):
+            cols = slice(n * OUTC, (n + 1) * OUTC)
+            res = sb.tile([P, OUTC], F32, name="res%d" % n)
+            nc.vector.scalar_tensor_tensor(res[:], old_t[:, cols], fade_t[:], placed[:, cols], ALU.mult, ALU.add)
+            eng = nc.sync if n % 2 == 0 else nc.scalar
+            eng.dma_start(out=out[:, cols], in_=res[:])

@@ -37,7 +37,7 @@ def tile_attend_quotaratio_stepwise_counts_heads_kernel(
         list2 = sb.tile([P, I // 16], U16, name="list2")
         list3 = sb.tile([P, I // 16], U16, name="list3")
         key_words = [sb.tile([P, T // 2], U32, name="key_words%d" % j, align_bytes=64) for j in range(2)]
-        key_scales = sb.tile([P, T], U8, name="key_scales", align_bytes=64)
+        key_scales = sb.tile([P, NB], U8, name="key_scales", align_bytes=64)
         raw = [sb.tile([P, PACK, Q], F32, name="raw%d" % j) for j in range(2)]
         lam_t = sb.tile([P, 1], F32, name="lam_t")
         pull_t = sb.tile([P, 1], F32, name="pull_t")
@@ -48,33 +48,29 @@ def tile_attend_quotaratio_stepwise_counts_heads_kernel(
 
         nc.vector.memset(key_scales[:].bitcast(I32), 0)
         nc.sync.dma_start(out=raw[0][:], in_=query.rearrange("(p j) w -> p j w", j=PACK))
-        for g in range(4):
-            nc.scalar.dma_start(
-                out=key_scales[32 * g : 32 * g + 4, :].bitcast(I32),
-                in_=keys_scales[0, 4 * g : 4 * g + 4, :].bitcast(I32),
-            )
         words_hbm = keys_words[0].rearrange("p n t -> p (n t)").bitcast(I32)
         nc.sync.dma_start(out=key_words[0][:].bitcast(I32), in_=words_hbm[:, 0 : T // 2])
+        for g in range(4):
+            nc.sync.dma_start(
+                out=key_scales[32 * g : 32 * g + 16, :].bitcast(I32),
+                in_=keys_scales[0, 4 * g : 4 * g + 4, :].bitcast(I32).rearrange("j (n c) -> n j c", n=T // NB),
+            )
         nc.sync.dma_start(out=raw[1][:], in_=query2.rearrange("(p j) w -> p j w", j=PACK))
         nc.sync.dma_start(out=key_words[1][:].bitcast(I32), in_=words_hbm[:, T // 2 : T])
         nc.sync.dma_start(list1[:], offs)
         nc.sync.dma_start(list2[:], offs2)
         nc.sync.dma_start(list3[:], offs3)
-        nc.gpsimd.dma_start(out=pull_t[:], in_=pull)
-        nc.gpsimd.dma_start(out=lam_t[:], in_=lam)
-        nc.gpsimd.dma_start(out=fade_t[:], in_=fade)
+        nc.sync.dma_start(out=lam_t[:], in_=lam)
+        nc.sync.dma_start(out=pull_t[:], in_=pull)
+        nc.sync.dma_start(out=fade_t[:], in_=fade)
         nc.sync.dma_start(out=old_t[:], in_=old)
         nc.vector.memset(placed[:], 0.0)
         nc.vector.memset(p_pad[:, 0:1], 0.0)
 
-        neg_pull = sb.tile([P, 1], F32, name="neg_pull")
-        nc.scalar.activation(neg_pull[:], pull_t[:], ACT.Copy, scale=-1.0)
         half_sign = sb.tile([P, 1], F32, name="half_sign")
-        nc.gpsimd.tensor_scalar(half_sign[:], lam_t[:], 0.0, -0.5, ALU.is_ge, ALU.add)
+        nc.gpsimd.tensor_scalar(half_sign[:], lam_t[:], 0.0, -0.5, ALU.is_lt, ALU.add)
         gain = sb.tile([P, 1], F32, name="gain")
         nc.gpsimd.tensor_tensor(gain[:], lam_t[:], half_sign[:], ALU.mult)
-        neg_gain = sb.tile([P, 1], F32, name="neg_gain")
-        nc.gpsimd.tensor_scalar(neg_gain[:], gain[:], -1.0, 0.0, ALU.mult, ALU.add)
 
         scores = []
         for j in range(2):
@@ -97,7 +93,7 @@ def tile_attend_quotaratio_stepwise_counts_heads_kernel(
                     lhsT=codes[:].bitcast(FP8X4),
                     lhsT_scale=qscales[:],
                     rhs=key_words[n // 2][:, (n % 2) * NB : (n % 2 + 1) * NB].bitcast(FP8X4),
-                    rhs_scale=key_scales[:, cols],
+                    rhs_scale=key_scales[4 * n : P, :],
                     start=True,
                     stop=True,
                 )
@@ -111,72 +107,65 @@ def tile_attend_quotaratio_stepwise_counts_heads_kernel(
         def entries(lst, h):
             return lst[:, h * (HALF // 16) : (h + 1) * (HALF // 16)]
 
-        own = [sb.tile([P, HALF], F32, name="own%d" % h) for h in range(2)]
-        diff = [sb.tile([P, 2, HALF], F32, name="diff%d" % h) for h in range(2)]
-        ex = [sb.tile([P, 2, HALF], F32, name="ex%d" % h) for h in range(2)]
+        halves = range(2)
+        own = [sb.tile([P, HALF], F32, name="own%d" % h) for h in halves]
         third = sb.tile([P, HALF], F32, name="third")
-
+        diff2 = [sb.tile([P, HALF], F32, name="diff2_%d" % h) for h in halves]
+        diff3 = [sb.tile([P, HALF], F32, name="diff3_%d" % h) for h in halves]
+        exp2 = [sb.tile([P, HALF], F32, name="exp2_%d" % h) for h in halves]
+        exp3 = [sb.tile([P, HALF], F32, name="exp3_%d" % h) for h in halves]
         nc.vector.tensor_copy(own[0][:], a[:].indirect(entries(list1, 0)))
-        nc.vector.tensor_tensor(diff[0][:, 0, :], a[:].indirect(entries(list2, 0)), own[0][:], ALU.subtract)
         nc.scalar.activation(own[1][:], a[:].indirect(entries(list1, 1)), ACT.Copy)
-        nc.vector.tensor_tensor(diff[0][:, 1, :], b[:].indirect(entries(list3, 0)), own[0][:], ALU.subtract)
-        nc.scalar.activation(ex[0][:, 0, :], diff[0][:, 0, :], ACT.Exp)
-        nc.scalar.activation(ex[0][:, 1, :], diff[0][:, 1, :], ACT.Exp)
-        nc.vector.tensor_tensor(diff[1][:, 0, :], a[:].indirect(entries(list2, 1)), own[1][:], ALU.subtract)
         nc.scalar.activation(third[:], b[:].indirect(entries(list3, 1)), ACT.Copy)
-        nc.scalar.activation(ex[1][:, 0, :], diff[1][:, 0, :], ACT.Exp)
+        nc.vector.tensor_tensor(diff2[0][:], a[:].indirect(entries(list2, 0)), own[0][:], ALU.subtract)
+        nc.vector.tensor_tensor(diff3[0][:], b[:].indirect(entries(list3, 0)), own[0][:], ALU.subtract)
+        nc.vector.tensor_tensor(diff2[1][:], a[:].indirect(entries(list2, 1)), own[1][:], ALU.subtract)
+        nc.vector.tensor_tensor(diff3[1][:], third[:], own[1][:], ALU.subtract)
+        for h in halves:
+            nc.scalar.activation(exp2[h][:], diff2[h][:], ACT.Exp)
+            nc.scalar.activation(exp3[h][:], diff3[h][:], ACT.Exp)
 
-        den = sb.tile([P, I], F32, name="den")
-        total = [sb.tile([P, HALF], F32, name="total%d" % h) for h in range(2)]
-        pair = [sb.tile([P, 2, QUART], F32, name="pair%d" % h) for h in range(2)]
-        quad = [sb.tile([P, QUART + h], F32, name="quad%d" % h) for h in range(2)]
-        inv_quad = [sb.tile([P, QUART + h], F32, name="inv_quad%d" % h) for h in range(2)]
-        inv_pair = [sb.tile([P, 2, QUART], F32, name="inv_pair%d" % h) for h in range(2)]
-        inv_den = [sb.tile([P, 2, 2 * QUART], F32, name="inv_den%d" % h) for h in range(2)]
-
-        def den_half(h):
-            return den[:, h * HALF : (h + 1) * HALF].rearrange("p (u n) -> p u n", u=2)
-
-        def make_den(h):
-            nc.vector.scalar_tensor_tensor(total[h][:], ex[h][:, 0, :], 1.0, ex[h][:, 1, :], ALU.add, ALU.add)
-            nc.vector.tensor_scalar(den[:, h * HALF : (h + 1) * HALF], total[h][:], CAP, half_sign[:], ALU.min, ALU.mult)
-
-        def fold(h):
-            dh = den_half(h)
-            nc.vector.tensor_tensor(pair[h][:].rearrange("p v n -> p (v n)"), dh[:, 0, :], dh[:, 1, :], ALU.mult)
+        den = sb.tile([P, 2, 2, 2, QUART], F32, name="den")
+        total = [sb.tile([P, HALF], F32, name="total%d" % h) for h in halves]
+        pair = [sb.tile([P, 2, QUART], F32, name="pair%d" % h) for h in halves]
+        quad = [sb.tile([P, QUART + 1 - h], F32, name="quad%d" % h) for h in halves]
+        inv_quad = [sb.tile([P, QUART + 1 - h], F32, name="inv_quad%d" % h) for h in halves]
+        others = [sb.tile([P, 2, 2, QUART], F32, name="others%d" % h) for h in halves]
+        inv_den = [sb.tile([P, 4, QUART], F32, name="inv_den%d" % h) for h in halves]
+        for h in halves:
+            nc.vector.scalar_tensor_tensor(total[h][:], exp2[h][:], 1.0, exp3[h][:], ALU.add, ALU.add)
+        for h in halves:
+            nc.vector.tensor_scalar(
+                den[:, h].rearrange("p u v n -> p (u v n)"), total[h][:], CAP, half_sign[:], ALU.min, ALU.mult
+            )
+        for h in halves:
+            nc.vector.tensor_tensor(pair[h][:], den[:, h, 0], den[:, h, 1], ALU.mult)
+        nc.vector.tensor_reduce(
+            quad[0][:, QUART : QUART + 1], den[:].rearrange("p h u v n -> p (h u v n)"), AX.X, ALU.max, negate=True
+        )
+        for h in halves:
             nc.vector.tensor_tensor(quad[h][:, 0:QUART], pair[h][:, 0, :], pair[h][:, 1, :], ALU.mult)
-
-        def unfold(h):
+        for h in halves:
             nc.vector.tensor_tensor(
-                inv_pair[h][:],
-                inv_quad[h][:, 0:QUART].unsqueeze(1).to_broadcast([P, 2, QUART]),
-                pair[h][:, ::-1, :],
+                others[h][:],
+                den[:, h, ::-1],
+                pair[h][:, ::-1, :].unsqueeze(1).to_broadcast([P, 2, 2, QUART]),
                 ALU.mult,
             )
+            nc.vector.reciprocal(inv_quad[h][:], quad[h][:])
+        neg_max = sb.tile([P, 1], F32, name="neg_max")
+        nc.scalar.activation(neg_max[:], inv_quad[0][:, QUART : QUART + 1], ACT.Copy, scale=gain[:])
+        for h in halves:
             nc.vector.tensor_tensor(
                 inv_den[h][:],
-                inv_pair[h][:].rearrange("p v n -> p (v n)").unsqueeze(1).to_broadcast([P, 2, 2 * QUART]),
-                den_half(h)[:, ::-1, :],
+                others[h][:].rearrange("p u v n -> p (u v) n"),
+                inv_quad[h][:, 0:QUART].unsqueeze(1).to_broadcast([P, 4, QUART]),
                 ALU.mult,
             )
 
-        make_den(0)
-        nc.vector.tensor_tensor(diff[1][:, 1, :], third[:], own[1][:], ALU.subtract)
-        nc.scalar.activation(ex[1][:, 1, :], diff[1][:, 1, :], ACT.Exp)
-        fold(0)
-        nc.vector.reciprocal(inv_quad[0][:], quad[0][:])
-        make_den(1)
-        fold(1)
-        nc.vector.tensor_reduce(quad[1][:, QUART : QUART + 1], den[:], AX.X, ALU.min)
-        unfold(0)
-        nc.vector.reciprocal(inv_quad[1][:], quad[1][:])
-        neg_max = sb.tile([P, 1], F32, name="neg_max")
-        nc.scalar.activation(neg_max[:], inv_quad[1][:, QUART : QUART + 1], ACT.Copy, scale=neg_gain[:])
-        unfold(1)
-
         sums = sb.tile([P, 2], F32, name="sums")
-        step = [sb.tile([P, HALF], F32, name="step%d" % h) for h in range(2)]
-        for h in range(2):
+        step = sb.tile([P, I], F32, name="step")
+        for h in halves:
             nc.scalar.activation(
                 p_pad[:, 1 + h * HALF : 1 + (h + 1) * HALF],
                 inv_den[h][:].rearrange("p u n -> p (u n)"),
@@ -185,23 +174,26 @@ def tile_attend_quotaratio_stepwise_counts_heads_kernel(
                 scale=gain[:],
                 accum_out=sums[:, h : h + 1],
             )
+
+        def step_half(h):
             nc.vector.scalar_tensor_tensor(
-                step[h][:],
+                step[:, h * HALF : (h + 1) * HALF],
                 p_pad[:, h * HALF : (h + 1) * HALF],
-                neg_pull[:],
+                pull_t[:],
                 p_pad[:, 1 + h * HALF : 1 + (h + 1) * HALF],
                 ALU.mult,
-                ALU.add,
+                ALU.subtract,
             )
+
+        step_half(0)
         row_sum = sb.tile([P, 1], F32, name="row_sum")
-        nc.vector.tensor_scalar(row_sum[:], sums[:, 0:1], sums[:, 1:2], 1.0 / 256.0, ALU.add, ALU.mult)
+        nc.vector.tensor_scalar(row_sum[:], sums[:, 0:1], sums[:, 1:2], -1.0 / 256.0, ALU.add, ALU.mult)
+        step_half(1)
         norm = sb.tile([P, 1], F32, name="norm")
         nc.vector.reciprocal(norm[:], row_sum[:])
-        ws = [sb.tile([P, HALF], F32, name="ws%d" % h) for h in range(2)]
-        nc.vector.tensor_scalar(ws[0][:], step[0][:], norm[:], None, ALU.mult)
-        nc.scalar.activation(ws[1][:], step[1][:], ACT.Copy, scale=norm[:])
-        for h in range(2):
-            nc.vector.tensor_copy(placed[:].indirect(entries(list1, h)), ws[h][:])
+        ws = sb.tile([P, I], F32, name="ws")
+        nc.vector.tensor_scalar(ws[:], step[:], norm[:], None, ALU.mult)
+        nc.vector.tensor_copy(placed[:].indirect(list1[:]), ws[:])
 
         for n in range(T // OUTC):
             cols = slice(n * OUTC, (n + 1) * OUTC)

from contextlib import ExitStack

import concourse.mybir as mybir

D, T, I, Q = 512, 1024, 512, 128
FLOPS = 2 * 2 * D * T * Q

F32 = mybir.dt.float32
BF16 = mybir.dt.bfloat16
I32 = mybir.dt.int32
U32 = mybir.dt.uint32
U16 = mybir.dt.uint16
U8 = mybir.dt.uint8
FP8X4 = mybir.dt.float8_e4m3fn_x4
ALU = mybir.AluOpType
ACT = mybir.ActivationFunctionType
AX = mybir.AxisListType

P = 128
PACK = 4
NB = 256
HALF = I // 2
QUART = HALF // 4
CAP = 2.0 ** 30
OUTC = 256


def tile_attend_quotaratio_stepwise_counts_heads_kernel(
    tc, query, query2, keys_words, keys_scales, lam, pull, old, fade, offs, offs2, offs3, out
):
    nc = tc.nc
    with ExitStack() as ctx:
        sb = ctx.enter_context(tc.tile_pool(name="sb", bufs=1))
        ps = ctx.enter_context(tc.psum_pool(name="ps", bufs=1))

        list1 = sb.tile([P, I // 16], U16, name="list1")
        list2 = sb.tile([P, I // 16], U16, name="list2")
        list3 = sb.tile([P, I // 16], U16, name="list3")
        key_words = [sb.tile([P, T // 2], U32, name="key_words%d" % j, align_bytes=64) for j in range(2)]
        key_scales = sb.tile([P, NB], U8, name="key_scales", align_bytes=64)
        raw = [sb.tile([P, PACK, Q], F32, name="raw%d" % j) for j in range(2)]
        lam_t = sb.tile([P, 1], F32, name="lam_t")
        pull_t = sb.tile([P, 1], F32, name="pull_t")
        fade_t = sb.tile([P, 1], F32, name="fade_t")
        old_t = sb.tile([P, T], F32, name="old_t")
        placed = sb.tile([P, T], F32, name="placed")
        p_pad = sb.tile([P, I + 1], F32, name="p_pad")

        nc.vector.memset(key_scales[:].bitcast(I32), 0)
        nc.sync.dma_start(out=raw[0][:], in_=query.rearrange("(p j) w -> p j w", j=PACK))
        words_hbm = keys_words[0].rearrange("p n t -> p (n t)").bitcast(I32)
        nc.sync.dma_start(out=key_words[0][:].bitcast(I32), in_=words_hbm[:, 0 : T // 2])
        for g in range(4):
            nc.sync.dma_start(
                out=key_scales[32 * g : 32 * g + 16, :].bitcast(I32),
                in_=keys_scales[0, 4 * g : 4 * g + 4, :].bitcast(I32).rearrange("j (n c) -> n j c", n=T // NB),
            )
        nc.sync.dma_start(out=raw[1][:], in_=query2.rearrange("(p j) w -> p j w", j=PACK))
        nc.sync.dma_start(out=key_words[1][:].bitcast(I32), in_=words_hbm[:, T // 2 : T])
        nc.sync.dma_start(list1[:], offs)
        nc.sync.dma_start(list2[:], offs2)
        nc.sync.dma_start(list3[:], offs3)
        nc.sync.dma_start(out=lam_t[:], in_=lam)
        nc.sync.dma_start(out=pull_t[:], in_=pull)
        nc.sync.dma_start(out=fade_t[:], in_=fade)
        nc.sync.dma_start(out=old_t[:], in_=old)
        nc.vector.memset(placed[:], 0.0)
        nc.vector.memset(p_pad[:, 0:1], 0.0)

        half_sign = sb.tile([P, 1], F32, name="half_sign")
        nc.gpsimd.tensor_scalar(half_sign[:], lam_t[:], 0.0, -0.5, ALU.is_lt, ALU.add)
        gain = sb.tile([P, 1], F32, name="gain")
        nc.gpsimd.tensor_tensor(gain[:], lam_t[:], half_sign[:], ALU.mult)

        scores = []
        for j in range(2):
            grouped = sb.tile([P, Q, PACK], BF16, name="grouped%d" % j, align_bytes=64)
            nc.vector.tensor_copy(
                out=grouped[:].rearrange("p (c i) t -> p c t i", i=4),
                in_=raw[j][:].rearrange("p t (c i) -> p c t i", i=4),
            )
            codes = sb.tile([P, Q], U32, name="codes%d" % j, align_bytes=64)
            qscales = sb.tile([P, Q], U8, name="qscales%d" % j, align_bytes=64)
            nc.vector.quantize_mx(
                out=codes[:].bitcast(FP8X4), scales=qscales[:], in_=grouped[:].rearrange("p w j -> p (w j)")
            )
            whole = sb.tile([P, T], F32, name="whole%d" % j)
            for n in range(T // NB):
                cols = slice(n * NB, (n + 1) * NB)
                bank = ps.tile([P, NB], F32, name="bank%d_%d" % (j, n))
                nc.tensor.matmul_mx(
                    out=bank[:],
                    lhsT=codes[:].bitcast(FP8X4),
                    lhsT_scale=qscales[:],
                    rhs=key_words[n // 2][:, (n % 2) * NB : (n % 2 + 1) * NB].bitcast(FP8X4),
                    rhs_scale=key_scales[4 * n : P, :],
                    start=True,
                    stop=True,
                )
                if j == 0 and n % 2 == 1:
                    nc.vector.tensor_copy(out=whole[:, cols], in_=bank[:])
                else:
                    nc.scalar.copy(whole[:, cols], bank[:])
            scores.append(whole)
        a, b = scores

        def entries(lst, h):
            return lst[:, h * (HALF // 16) : (h + 1) * (HALF // 16)]

        halves = range(2)
        own = [sb.tile([P, HALF], F32, name="own%d" % h) for h in halves]
        third = sb.tile([P, HALF], F32, name="third")
        diff2 = [sb.tile([P, HALF], F32, name="diff2_%d" % h) for h in halves]
        diff3 = [sb.tile([P, HALF], F32, name="diff3_%d" % h) for h in halves]
        exp2 = [sb.tile([P, HALF], F32, name="exp2_%d" % h) for h in halves]
        exp3 = [sb.tile([P, HALF], F32, name="exp3_%d" % h) for h in halves]
        nc.vector.tensor_copy(own[0][:], a[:].indirect(entries(list1, 0)))
        nc.scalar.activation(own[1][:], a[:].indirect(entries(list1, 1)), ACT.Copy)
        nc.scalar.activation(third[:], b[:].indirect(entries(list3, 1)), ACT.Copy)
        nc.vector.tensor_tensor(diff2[0][:], a[:].indirect(entries(list2, 0)), own[0][:], ALU.subtract)
        nc.vector.tensor_tensor(diff3[0][:], b[:].indirect(entries(list3, 0)), own[0][:], ALU.subtract)
        nc.vector.tensor_tensor(diff2[1][:], a[:].indirect(entries(list2, 1)), own[1][:], ALU.subtract)
        nc.vector.tensor_tensor(diff3[1][:], third[:], own[1][:], ALU.subtract)
        for h in halves:
            nc.scalar.activation(exp2[h][:], diff2[h][:], ACT.Exp)
            nc.scalar.activation(exp3[h][:], diff3[h][:], ACT.Exp)

        den = sb.tile([P, 2, 2, 2, QUART], F32, name="den")
        total = [sb.tile([P, HALF], F32, name="total%d" % h) for h in halves]
        pair = [sb.tile([P, 2, QUART], F32, name="pair%d" % h) for h in halves]
        quad = [sb.tile([P, QUART + 1 - h], F32, name="quad%d" % h) for h in halves]
        inv_quad = [sb.tile([P, QUART + 1 - h], F32, name="inv_quad%d" % h) for h in halves]
        others = [sb.tile([P, 2, 2, QUART], F32, name="others%d" % h) for h in halves]
        inv_den = [sb.tile([P, 4, QUART], F32, name="inv_den%d" % h) for h in halves]
        for h in halves:
            nc.vector.scalar_tensor_tensor(total[h][:], exp2[h][:], 1.0, exp3[h][:], ALU.add, ALU.add)
        for h in halves:
            nc.vector.tensor_scalar(
                den[:, h].rearrange("p u v n -> p (u v n)"), total[h][:], CAP, half_sign[:], ALU.min, ALU.mult
            )
        for h in halves:
            nc.vector.tensor_tensor(pair[h][:], den[:, h, 0], den[:, h, 1], ALU.mult)
        nc.vector.tensor_reduce(
            quad[0][:, QUART : QUART + 1], den[:].rearrange("p h u v n -> p (h u v n)"), AX.X, ALU.max, negate=True
        )
        for h in halves:
            nc.vector.tensor_tensor(quad[h][:, 0:QUART], pair[h][:, 0, :], pair[h][:, 1, :], ALU.mult)
        for h in halves:
            nc.vector.tensor_tensor(
                others[h][:],
                den[:, h, ::-1],
                pair[h][:, ::-1, :].unsqueeze(1).to_broadcast([P, 2, 2, QUART]),
                ALU.mult,
            )
            nc.vector.reciprocal(inv_quad[h][:], quad[h][:])
        neg_max = sb.tile([P, 1], F32, name="neg_max")
        nc.scalar.activation(neg_max[:], inv_quad[0][:, QUART : QUART + 1], ACT.Copy, scale=gain[:])
        for h in halves:
            nc.vector.tensor_tensor(
                inv_den[h][:],
                others[h][:].rearrange("p u v n -> p (u v) n"),
                inv_quad[h][:, 0:QUART].unsqueeze(1).to_broadcast([P, 4, QUART]),
                ALU.mult,
            )

        sums = sb.tile([P, 2], F32, name="sums")
        step = sb.tile([P, I], F32, name="step")
        for h in halves:
            nc.scalar.activation(
                p_pad[:, 1 + h * HALF : 1 + (h + 1) * HALF],
                inv_den[h][:].rearrange("p u n -> p (u n)"),
                ACT.Exp,
                bias=neg_max[:],
                scale=gain[:],
                accum_out=sums[:, h : h + 1],
            )

        def step_half(h):
            nc.vector.scalar_tensor_tensor(
                step[:, h * HALF : (h + 1) * HALF],
                p_pad[:, h * HALF : (h + 1) * HALF],
                pull_t[:],
                p_pad[:, 1 + h * HALF : 1 + (h + 1) * HALF],
                ALU.mult,
                ALU.subtract,
            )

        step_half(0)
        row_sum = sb.tile([P, 1], F32, name="row_sum")
        nc.vector.tensor_scalar(row_sum[:], sums[:, 0:1], sums[:, 1:2], -1.0 / 256.0, ALU.add, ALU.mult)
        step_half(1)
        norm = sb.tile([P, 1], F32, name="norm")
        nc.vector.reciprocal(norm[:], row_sum[:])
        ws = sb.tile([P, I], F32, name="ws")
        nc.vector.tensor_scalar(ws[:], step[:], norm[:], None, ALU.mult)
        nc.vector.tensor_copy(placed[:].indirect(list1[:]), ws[:])

        for n in range(T // OUTC):
            cols = slice(n * OUTC, (n + 1) * OUTC)
            res = sb.tile([P, OUTC], F32, name="res%d" % n)
            nc.vector.scalar_tensor_tensor(res[:], old_t[:, cols], fade_t[:], placed[:, cols], ALU.mult, ALU.add)
            eng = nc.sync if n % 2 == 0 else nc.scalar
            eng.dma_start(out=out[:, cols], in_=res[:])
